import numpy as np
CORES = [52,68,84,180,196,212,308,324,340]
N = 9
W, KW, DIL = 128, 3, 8
H = (KW // 2) * DIL
def setup_inputs(rng):
    return {"x": rng.standard_normal((N, 128, W), dtype=np.float32), "w": rng.standard_normal((N, 128, KW * 128), dtype=np.float32)}
def setup_inputs_big(rng):
    d = setup_inputs(rng)
    for k in ("x", "w"): d[k] = (d[k].astype(np.float32) * 1024.0).astype(d[k].dtype)
    return d
def setup_inputs_small(rng):
    d = setup_inputs(rng)
    for k in ("x", "w"): d[k] = (d[k].astype(np.float32) * (1 / 1024.0)).astype(d[k].dtype)
    return d
def setup_inputs_apart(rng):
    d = setup_inputs(rng)
    f = (10.0 ** rng.permutation(np.linspace(-1.5, 1.5, N))).astype(np.float32).reshape(N, 1, 1)
    for k in ("x", "w"): d[k] = (d[k].astype(np.float32) * f).astype(d[k].dtype)
    return d
def reference(x, w):
    X, W_ = x.astype(np.float64), w.astype(np.float64)
    g = np.concatenate(list(X), axis=1)
    p = np.concatenate([g[:, -H:], g, g[:, :H]], axis=1)
    y = np.zeros((N, 128, W))
    for r in range(N):
        for i in range(KW):
            y[r] += W_[r][:, 128 * i:128 * i + 128].T @ p[:, W * r + i * DIL:W * r + i * DIL + W]
    return {"y": y.astype(np.float32 if x.dtype != np.float64 else np.float64)}

from concourse.bass import DstId, RemoteDMATransfer

P = 128
W, KW, DIL = 128, 3, 8
H = (KW // 2) * DIL

SCRATCH = {
    "xs": ("sbuf", [P, H + W + H], "float32"),
    "ws": ("sbuf", [P, KW * P], "float32"),
    "ys": ("sbuf", [P, W], "float32"),
    "pk": ("dram", [P, H], "float32"),
    "rl": ("dram", [P, H], "float32"),
    "pm": ("psum", [P, 512], "float32"),
    "pl": ("psum", [P, 512], "float32"),
    "pr": ("psum", [P, 512], "float32"),
}
SEMAPHORES = ["e0", "e1", "xm", "wl",
              "h0", "h1", "rin", "sent",
              "m0", "m1", "mm", "c0", "c1", "cm", "s0", "s1", "sm"]


def _bits(mask):
    return [1 << b for b in range(mask.bit_length()) if (mask >> b) & 1]


def _plan(cores, topo):
    n = len(cores)

    def one_link(a, b):
        return topo.same_plane(a, b) or topo.mates(a, b) or topo.chip(a) == topo.chip(b)

    routes, used = {}, []
    for r in range(n):
        for side in (0, 1):
            d = (r + (1 if side else -1)) % n
            if topo.may_write(cores[r], cores[d]):
                routes[(r, side)] = None
                continue
            cands = [m for m in range(n) if m != r and m != d and m not in used
                     and topo.may_write(cores[r], cores[m]) and topo.may_write(cores[m], cores[d])]
            best = min(cands, key=lambda m: (not one_link(cores[r], cores[m])) + (not one_link(cores[m], cores[d])))
            used.append(best)
            routes[(r, side)] = best
    return routes


def rank_program(g, core, T, topo):
    rank = T.rank_of(core)
    if rank is None:
        return
    cores = list(T.cores)
    n = len(cores)
    routes = _plan(cores, topo)
    S = T.sem

    def nb(r, side):
        return (r + (1 if side else -1)) % n

    def last_mask(s, side):
        d = cores[nb(s, side)]
        m = routes[(s, side)]
        if m is not None:
            return topo.mask(cores[m], d)
        if routes[(s, 1 - side)] is not None:
            return topo.mask(cores[s], d)
        both = _bits(topo.mask(cores[s], d) & topo.mask(cores[s], cores[nb(s, 1 - side)]))
        half = len(both) // 2
        return sum(both[half:] if side else both[:half])

    e_sem = (S.e0, S.e1)
    h_sem = (S.h0, S.h1)
    x_edge = (T.x[:, 0:H], T.x[:, W - H:W])
    s_edge = (T.xs[:, H:2 * H], T.xs[:, W:W + H])
    halo = (T.xs[:, 0:H], T.xs[:, H + W:H + W + H])
    far = [side for side in (0, 1) if routes[(rank, side)] is not None]

    order = far + [side for side in (0, 1) if side not in far]
    for q, side in zip((g.sync, g.scalar), order):
        q.dma_start(T.pk[:] if side in far else s_edge[side], x_edge[side]).then_inc(e_sem[side], 16)
    lo = 0 if 0 in far else H
    hi = W if 1 in far else W - H
    g.sync.dma_start(T.xs[:, H + lo:H + hi], T.x[:, lo:hi]).then_inc(S.xm, 16)
    g.scalar.dma_start(T.ws[:], T.w[:]).then_inc(S.wl, 16)

    sent = 0
    if far:
        for side in order:
            g.wait_ge(e_sem[side], 16)
            if side in far:
                d = cores[routes[(rank, side)]]
                rid, pid = topo.addr(d, core)
                mask = _bits(topo.mask(core, d))[0]
                g.remote_dma(T.rl[:], T.pk[:], S.rin, S.sent, pid, rid, mask)
            else:
                d = cores[nb(rank, side)]
                rid, pid = topo.addr(d, core)
                mask = last_mask(rank, side)
                g.remote_dma(halo[1 - side], s_edge[side], h_sem[1 - side], S.sent, pid, rid, mask)
            sent += len(_bits(mask))
    else:
        trs = []
        for side in (0, 1):
            g.wait_ge(e_sem[side], 16)
            rid, pid = topo.addr(cores[nb(rank, side)], core)
            mask = last_mask(rank, side)
            trs.append(RemoteDMATransfer(dst_ids=[DstId(rid=rid, pnc=pid)], dma_engine_mask=mask,
                                         remote_sem=h_sem[1 - side], src=s_edge[side], dst=halo[1 - side]))
            sent += len(_bits(mask))
        g.remote_dma_fused(trs, local_sem=S.sent)
    for (s, side), m in routes.items():
        if m == rank:
            first = len(_bits(_bits(topo.mask(cores[s], core))[0]))
            g.wait_ge(S.rin, first)
            d = cores[nb(s, side)]
            rid, pid = topo.addr(d, core)
            mask = last_mask(s, side)
            g.remote_dma(halo[1 - side], T.rl[:], h_sem[1 - side], S.sent, pid, rid, mask)
            sent += len(_bits(mask))
    g.wait_ge(S.sent, sent)

    def mm(ps, a, b, i, start, stop):
        return g.tensor.matmul(ps[:, 0:b - a], T.ws[:, P * i:P * (i + 1)], T.xs[:, a + DIL * i:b + DIL * i], start, stop)

    t = g.tensor
    for side in (0, 1):
        if side not in far:
            t.wait_ge(e_sem[side], 16)
    t.wait_ge(S.xm, 16)
    t.wait_ge(S.wl, 16)
    blocks = ((T.pl, 0, H, 0, S.m0, S.c0, S.s0), (T.pr, W - H, W, KW - 1, S.m1, S.c1, S.s1))
    for i in range(KW):
        ins = mm(T.pm, H, W - H, i, i == 0, i == KW - 1)
    ins.then_inc(S.mm, 1)
    for ps, a, b, tap, _m, _c, _s in blocks:
        local = [i for i in range(KW) if i != tap]
        for i in local:
            mm(ps, a, b, i, i == local[0], False)
    take = sorted((0, 1), key=lambda k: routes[(nb(rank, k), 1 - k)] is not None)
    for k in take:
        ps, a, b, tap, m_sem, _c, _s = blocks[k]
        t.wait_ge(h_sem[k], len(_bits(last_mask(nb(rank, k), 1 - k))))
        mm(ps, a, b, tap, False, True).then_inc(m_sem, 1)

    v = g.vector
    v.wait_ge(S.mm, 1)
    v.tensor_copy(T.ys[:, H:W - H], T.pm[:, 0:W - 2 * H]).then_inc(S.cm, 1)
    g.scalar.wait_ge(S.cm, 1)
    g.scalar.dma_start(T.y[:, H:W - H], T.ys[:, H:W - H]).then_inc(S.sm, 16)
    for q, k in zip((g.scalar, g.sync), take):
        ps, a, b, tap, m_sem, c_sem, s_sem = blocks[k]
        v.wait_ge(m_sem, 1)
        v.tensor_copy(T.ys[:, a:b], ps[:, 0:b - a]).then_inc(c_sem, 1)
        q.wait_ge(c_sem, 1)
        q.dma_start(T.y[:, a:b], T.ys[:, a:b]).then_inc(s_sem, 16)
    g.scalar.wait_ge(S.sm, 16)
    for q, k in zip((g.scalar, g.sync), take):
        q.wait_ge(blocks[k][6], 16)
